import numpy as np
import ml_dtypes


def mxq(x, axis, fmt="e4m3"):
    dtype, down = {"e4m3": (ml_dtypes.float8_e4m3fn, 7), "e5m2": (ml_dtypes.float8_e5m2, 14)}[fmt]
    v = np.moveaxis(np.asarray(x, np.float32).astype(ml_dtypes.bfloat16).astype(np.float64), axis, -1)
    blocks = v.reshape(v.shape[:-1] + (-1, 32))
    amax = np.abs(blocks).max(-1, keepdims=True)
    byte = np.maximum(np.where(amax > 0, np.frexp(amax)[1] - 1 + 127, 0) - down, 1)
    scale = np.exp2(byte - 127.0)
    codes = (blocks / scale).astype(np.float32).astype(dtype).astype(np.float64)
    return np.moveaxis((codes * scale).reshape(v.shape), -1, axis)


WIDE = False


def mx_kscale(k):
    if not WIDE:
        return np.ones(k)
    levels = np.array([10, -10, 5, -5, 0])
    if k % 512:
        return np.exp2(np.random.permutation(np.resize(levels, k // 32))).repeat(32)
    a = np.empty((k // 512, 16))
    for p in range(k // 512):
        a[p, :8] = np.random.permutation(np.resize(levels, 8))
        for g in range(8):
            far = levels[np.abs(levels - a[p, g]) >= 10]
            a[p, g + 8] = far[np.random.randint(len(far))]
    return np.exp2(a.ravel()).repeat(32)


def f64(x):
    return np.asarray(x).astype(np.float64)


def striped8(idx):
    return np.asarray(idx).reshape(8, -1, 16).transpose(0, 2, 1).reshape(128, -1).astype(np.uint16)


def unstriped8(offs):
    return offs.reshape(8, 16, -1).transpose(0, 2, 1).reshape(8, -1).astype(np.int64)


def pick8(x, idx, run):
    r = np.arange(len(x))
    return x[r[:, None], idx[r % (8 * run) // run]]


E2M1 = np.array([0.0, 0.5, 1.0, 1.5, 2.0, 3.0, 4.0, 6.0, -0.0, -0.5, -1.0, -1.5, -2.0, -3.0, -4.0, -6.0])


def pack_weight(w, fmt):
    k, n = w.shape
    w = f64(np.asarray(w, np.float32).astype(ml_dtypes.bfloat16)).reshape(k // 32, 32, n)
    amax = np.abs(w).max(1)
    if fmt == "e4m3":
        byte = np.frexp(amax)[1] - 1 + 127 - 7
    else:
        mant, ex = np.frexp(amax / 6.0)
        byte = np.where(mant > 0.5, ex, ex - 1) + 127
    byte = np.clip(np.where(amax > 0, byte, 1), 1, 254)
    scaled = (w * np.exp2(127.0 - byte)[:, None, :]).reshape(k, n).astype(np.float32)
    by_word = np.ascontiguousarray(scaled.reshape(k // 512, 128, 4, n).transpose(0, 1, 3, 2))
    if fmt == "e4m3":
        words = by_word.astype(ml_dtypes.float8_e4m3fn).view(np.uint8)
    else:
        c = by_word.astype(ml_dtypes.float4_e2m1fn).view(np.uint8) & 0xF
        words = (c[..., 0::2] | (c[..., 1::2] << 4)).reshape(k // 512, 128, 2 * n)
    return np.ascontiguousarray(words), np.ascontiguousarray(byte.astype(np.uint8).reshape(k // 512, 16, n))


def unpack_weight(words, scales, fmt):
    g, _, n = scales.shape
    words = np.ascontiguousarray(words).reshape(g, 128, n, -1)
    if fmt == "e4m3":
        vals = words.view(ml_dtypes.float8_e4m3fn).astype(np.float64)
    else:
        nib = np.empty((g, 128, n, 4), np.uint8)
        nib[..., 0::2] = words & 0xF
        nib[..., 1::2] = words >> 4
        vals = E2M1[nib]
    vals = vals * np.repeat(np.exp2(scales.astype(np.float64) - 127.0), 8, axis=1)[..., None]
    return vals.transpose(0, 1, 3, 2).reshape(g * 512, n)


D, T, U, I, O, L, Q = 512, 1024, 1024, 512, 2048, 1024, 128


def setup_inputs():
    n = np.random.standard_normal
    idx = np.stack([np.random.permutation(O)[:L] for _ in range(8)])
    idx2 = np.stack([np.random.permutation(O)[:L] for _ in range(8)])
    idx3 = np.stack([np.random.permutation(T)[:I] for _ in range(8)])
    idx4 = np.stack([np.random.permutation(U)[:I] for _ in range(8)])
    fd = mx_kscale(D)
    cachep = pack_weight(n((D, T)) / fd[:, None], "e4m3")
    draftp = pack_weight(n((D, U)) / fd[:, None], "e2m1")
    return {
        "query": (n((D, Q)) * 1.0 / np.sqrt(D) * fd[:, None]).astype(np.float32),
        "cache_words": cachep[0],
        "cache_scales": cachep[1],
        "draft_words": draftp[0],
        "draft_scales": draftp[1],
        "offs": striped8(idx),
        "offs2": striped8(idx2),
        "offs3": striped8(idx3),
        "offs4": striped8(idx4),
    }


def reference(query, cache_words, cache_scales, draft_words, draft_scales, offs, offs2, offs3, offs4):
    idx = unstriped8(offs)
    idx2 = unstriped8(offs2)
    idx3 = unstriped8(offs3)
    idx4 = unstriped8(offs4)
    cacheu = unpack_weight(cache_words, cache_scales, "e4m3")
    draftu = unpack_weight(draft_words, draft_scales, "e2m1")
    queryq = mxq(f64(query), 0, "e4m3")
    a = queryq.T @ cacheu
    b = queryq.T @ draftu
    ab = np.concatenate([a, b], axis=1)
    f1 = np.zeros((Q, O))
    f1[np.arange(Q)[:, None], idx2[np.arange(Q) % 128 // 16]] = pick8(ab, idx, 16)
    r = ab - f1
    aa = r[:, 0:0 + T]
    bb = r[:, 1024:1024 + U]
    y = np.maximum(pick8(aa, idx3, 16), pick8(bb, idx4, 16))
    return y

@@ -1,0 +1,135 @@
+from contextlib import ExitStack
+
+import concourse.mybir as mybir
+
+D, T, U, I, O, L, Q = 512, 1024, 1024, 512, 2048, 1024, 128
+FLOPS = 2 * D * Q * (T + U)
+
+F32 = mybir.dt.float32
+BF16 = mybir.dt.bfloat16
+I32 = mybir.dt.int32
+U32 = mybir.dt.uint32
+U16 = mybir.dt.uint16
+U8 = mybir.dt.uint8
+FP8X4 = mybir.dt.float8_e4m3fn_x4
+FP4X4 = mybir.dt.float4_e2m1fn_x4
+COPY = mybir.ActivationFunctionType.Copy
+SUB = mybir.AluOpType.subtract
+MAX = mybir.AluOpType.max
+
+P = 128
+PACK = 4
+N_TILE = 256
+CACHE_ROW = 4
+Q_VECTOR = 64
+
+
+def tile_attend_endandback_two_kernel(
+    tc, query, cache_words, cache_scales, draft_words, draft_scales, offs, offs2, offs3, offs4, out
+):
+    nc = tc.nc
+    with ExitStack() as ctx:
+        keep = ctx.enter_context(tc.tile_pool(name="keep", bufs=1))
+        psum = ctx.enter_context(tc.psum_pool(name="psum", bufs=1))
+
+        idx = keep.tile([P, L // 16], U16, name="idx")
+        idx2 = keep.tile([P, L // 16], U16, name="idx2")
+        idx3 = keep.tile([P, I // 16], U16, name="idx3")
+        idx4 = keep.tile([P, I // 16], U16, name="idx4")
+
+        draft_plane = keep.tile([P, U], U8, name="draft_plane", align_bytes=64)
+        cache_plane = keep.tile([P, T], U8, name="cache_plane", align_bytes=64)
+        nc.vector.memset(draft_plane[:].bitcast(I32), 0)
+        nc.vector.memset(cache_plane[:].bitcast(I32), 0)
+
+        q_raw = keep.tile([P, PACK, Q], F32, name="q_raw")
+        nc.sync.dma_start(out=q_raw[:], in_=query.rearrange("(p j) q -> p j q", j=PACK))
+        for r in range(4):
+            nc.sync.dma_start(
+                out=draft_plane[r:P:32, :].bitcast(I32), in_=draft_scales[0, r:16:4, :].bitcast(I32)
+            )
+        draft = keep.tile([P, 2 * U], U8, name="draft", align_bytes=64)
+        nc.sync.dma_start(out=draft[:].bitcast(I32), in_=draft_words[0].bitcast(I32))
+        cache = keep.tile([P, T], I32, name="cache", align_bytes=64)
+        nc.sync.dma_start(out=cache[:], in_=cache_words[0].rearrange("p n t -> p (n t)").bitcast(I32))
+        for r in range(4):
+            nc.sync.dma_start(
+                out=cache_plane[CACHE_ROW + r : P : 32, :].bitcast(I32),
+                in_=cache_scales[0, r:16:4, :].bitcast(I32),
+            )
+        nc.sync.dma_start(idx[:], offs)
+        nc.sync.dma_start(idx2[:], offs2)
+        nc.sync.dma_start(idx3[:], offs3)
+        nc.sync.dma_start(idx4[:], offs4)
+
+        f1 = keep.tile([P, O], F32, name="f1")
+        nc.vector.memset(f1[:], 0.0)
+
+        q_bf = keep.tile([P, Q, PACK], BF16, name="q_bf", align_bytes=64)
+        nc.vector.tensor_copy(
+            out=q_bf[:, 0:Q_VECTOR, :].rearrange("p (c i) t -> p c t i", i=4),
+            in_=q_raw[:, :, 0:Q_VECTOR].rearrange("p t (c i) -> p c t i", i=4),
+        )
+        nc.scalar.activation(
+            q_bf[:, Q_VECTOR:Q, :].rearrange("p (c i) t -> p c t i", i=4),
+            q_raw[:, :, Q_VECTOR:Q].rearrange("p t (c i) -> p c t i", i=4),
+            COPY,
+        )
+        q_codes = keep.tile([P, Q], U32, name="q_codes", align_bytes=64)
+        q_plane = keep.tile([P, Q], U8, name="q_plane", align_bytes=64)
+        nc.vector.quantize_mx(
+            out=q_codes[:].bitcast(FP8X4), scales=q_plane[:], in_=q_bf[:].rearrange("p q t -> p (q t)")
+        )
+
+        ab = keep.tile([P, O], F32, name="ab")
+        for s in range(O // N_TILE):
+            acc = psum.tile([P, N_TILE], F32, name="acc%d" % s)
+            if s < U // N_TILE:
+                c = s * N_TILE
+                rhs = draft[:, 2 * c : 2 * (c + N_TILE)].bitcast(FP4X4)
+                rhs_scale = draft_plane[:, c : c + N_TILE]
+                place = T + c
+            else:
+                c = s * N_TILE - U
+                rhs = cache[:, c : c + N_TILE].bitcast(FP8X4)
+                rhs_scale = cache_plane[CACHE_ROW:P, c : c + N_TILE]
+                place = c
+            nc.tensor.matmul_mx(
+                out=acc[:],
+                lhsT=q_codes[:].bitcast(FP8X4),
+                lhsT_scale=q_plane[:],
+                rhs=rhs,
+                rhs_scale=rhs_scale,
+                start=True,
+                stop=True,
+            )
+            if s % 2 == 0:
+                nc.scalar.activation(ab[:, place : place + N_TILE], acc[:], COPY)
+            else:
+                nc.vector.tensor_copy(ab[:, place : place + N_TILE], acc[:])
+
+        half = L // 2
+        for h in range(2):
+            picked = keep.tile([P, half], F32, name="picked%d" % h)
+            cols = slice(h * half // 16, (h + 1) * half // 16)
+            nc.vector.tensor_copy(picked[:], ab[:].indirect(idx[:, cols]))
+            nc.scalar.activation(f1[:].indirect(idx2[:, cols]), picked[:], COPY)
+
+        aa = keep.tile([P, T], F32, name="aa")
+        bb = keep.tile([P, U], F32, name="bb")
+        nc.vector.tensor_tensor(aa[:], ab[:, 0:T], f1[:, 0:T], SUB)
+        nc.vector.tensor_tensor(bb[:], ab[:, T:O], f1[:, T:O], SUB)
+
+        ga = keep.tile([P, I], F32, name="ga")
+        nc.scalar.activation(ga[:], aa[:].indirect(idx3[:]), COPY)
+        hi = I // 2
+        gb0 = keep.tile([P, hi], F32, name="gb0")
+        gb1 = keep.tile([P, hi], F32, name="gb1")
+        nc.scalar.activation(gb1[:], bb[:].indirect(idx4[:, hi // 16 : I // 16]), COPY)
+        nc.vector.tensor_copy(gb0[:], bb[:].indirect(idx4[:, 0 : hi // 16]))
+        y0 = keep.tile([P, hi], F32, name="y0")
+        nc.vector.tensor_tensor(y0[:], ga[:, 0:hi], gb0[:], MAX)
+        nc.scalar.dma_start(out=out[:, 0:hi], in_=y0[:])
+        y1 = keep.tile([P, hi], F32, name="y1")
+        nc.vector.tensor_tensor(y1[:], ga[:, hi:I], gb1[:], MAX)
+        nc.sync.dma_start(out=out[:, hi:I], in_=y1[:])

@@ -48,6 +48,7 @@ def tile_attend_endandback_two_kernel(
             nc.sync.dma_start(
                 out=draft_plane[r:P:32, :].bitcast(I32), in_=draft_scales[0, r:16:4, :].bitcast(I32)
             )
+        nc.sync.dma_start(idx[:], offs)
         draft = keep.tile([P, 2 * U], U8, name="draft", align_bytes=64)
         nc.sync.dma_start(out=draft[:].bitcast(I32), in_=draft_words[0].bitcast(I32))
         cache = keep.tile([P, T], I32, name="cache", align_bytes=64)
@@ -57,7 +58,6 @@ def tile_attend_endandback_two_kernel(
                 out=cache_plane[CACHE_ROW + r : P : 32, :].bitcast(I32),
                 in_=cache_scales[0, r:16:4, :].bitcast(I32),
             )
-        nc.sync.dma_start(idx[:], offs)
         nc.sync.dma_start(idx2[:], offs2)
         nc.sync.dma_start(idx3[:], offs3)
         nc.sync.dma_start(idx4[:], offs4)
@@ -82,6 +82,7 @@ def tile_attend_endandback_two_kernel(
         )
 
         ab = keep.tile([P, O], F32, name="ab")
+        banks = {}
         for s in range(O // N_TILE):
             acc = psum.tile([P, N_TILE], F32, name="acc%d" % s)
             if s < U // N_TILE:
@@ -103,22 +104,29 @@ def tile_attend_endandback_two_kernel(
                 start=True,
                 stop=True,
             )
-            if s % 2 == 0:
+            banks[place] = acc
+            if s % 2 == 1:
                 nc.scalar.activation(ab[:, place : place + N_TILE], acc[:], COPY)
             else:
                 nc.vector.tensor_copy(ab[:, place : place + N_TILE], acc[:])
 
         half = L // 2
-        for h in range(2):
-            picked = keep.tile([P, half], F32, name="picked%d" % h)
-            cols = slice(h * half // 16, (h + 1) * half // 16)
-            nc.vector.tensor_copy(picked[:], ab[:].indirect(idx[:, cols]))
-            nc.scalar.activation(f1[:].indirect(idx2[:, cols]), picked[:], COPY)
+        picked = keep.tile([P, L], F32, name="picked")
+        nc.scalar.activation(picked[:, 0:half], ab[:].indirect(idx[:, 0 : half // 16]), COPY)
+        nc.vector.tensor_copy(picked[:, half:L], ab[:].indirect(idx[:, half // 16 : L // 16]))
+        nc.scalar.activation(f1[:].indirect(idx2[:]), picked[:], COPY)
 
         aa = keep.tile([P, T], F32, name="aa")
         bb = keep.tile([P, U], F32, name="bb")
-        nc.vector.tensor_tensor(aa[:], ab[:, 0:T], f1[:, 0:T], SUB)
-        nc.vector.tensor_tensor(bb[:], ab[:, T:O], f1[:, T:O], SUB)
+        for part, base in ((aa, 0), (bb, T)):
+            last = T - N_TILE
+            nc.gpsimd.tensor_tensor(
+                part[:, last:T], ab[:, base + last : base + T], f1[:, base + last : base + T], SUB
+            )
+            for c in range(0, last, N_TILE):
+                nc.vector.tensor_tensor(
+                    part[:, c : c + N_TILE], banks[base + c][:], f1[:, base + c : base + c + N_TILE], SUB
+                )
 
         ga = keep.tile([P, I], F32, name="ga")
         nc.scalar.activation(ga[:], aa[:].indirect(idx3[:]), COPY)

@@ -21,7 +21,9 @@ P = 128
 PACK = 4
 N_TILE = 256
 CACHE_ROW = 4
-Q_VECTOR = 64
+Q_VECTOR = 80
+VECTOR_A = 768
+VECTOR_B = 640
 
 
 def tile_attend_endandback_two_kernel(
@@ -48,7 +50,6 @@ def tile_attend_endandback_two_kernel(
             nc.sync.dma_start(
                 out=draft_plane[r:P:32, :].bitcast(I32), in_=draft_scales[0, r:16:4, :].bitcast(I32)
             )
-        nc.sync.dma_start(idx[:], offs)
         draft = keep.tile([P, 2 * U], U8, name="draft", align_bytes=64)
         nc.sync.dma_start(out=draft[:].bitcast(I32), in_=draft_words[0].bitcast(I32))
         cache = keep.tile([P, T], I32, name="cache", align_bytes=64)
@@ -58,6 +59,7 @@ def tile_attend_endandback_two_kernel(
                 out=cache_plane[CACHE_ROW + r : P : 32, :].bitcast(I32),
                 in_=cache_scales[0, r:16:4, :].bitcast(I32),
             )
+        nc.sync.dma_start(idx[:], offs)
         nc.sync.dma_start(idx2[:], offs2)
         nc.sync.dma_start(idx3[:], offs3)
         nc.sync.dma_start(idx4[:], offs4)
@@ -118,14 +120,14 @@ def tile_attend_endandback_two_kernel(
 
         aa = keep.tile([P, T], F32, name="aa")
         bb = keep.tile([P, U], F32, name="bb")
-        for part, base in ((aa, 0), (bb, T)):
-            last = T - N_TILE
+        for part, base, share in ((aa, 0, VECTOR_A), (bb, T, VECTOR_B)):
             nc.gpsimd.tensor_tensor(
-                part[:, last:T], ab[:, base + last : base + T], f1[:, base + last : base + T], SUB
+                part[:, share:T], ab[:, base + share : base + T], f1[:, base + share : base + T], SUB
             )
-            for c in range(0, last, N_TILE):
+            for c in range(0, share, N_TILE):
+                n = min(N_TILE, share - c)
                 nc.vector.tensor_tensor(
-                    part[:, c : c + N_TILE], banks[base + c][:], f1[:, base + c : base + c + N_TILE], SUB
+                    part[:, c : c + n], banks[base + c][:, 0:n], f1[:, base + c : base + c + n], SUB
                 )
 
         ga = keep.tile([P, I], F32, name="ga")

@@ -139,7 +139,7 @@ def tile_attend_endandback_two_kernel(
         nc.vector.tensor_copy(gb0[:], bb[:].indirect(idx4[:, 0 : hi // 16]))
         y0 = keep.tile([P, hi], F32, name="y0")
         nc.vector.tensor_tensor(y0[:], ga[:, 0:hi], gb0[:], MAX)
-        nc.scalar.dma_start(out=out[:, 0:hi], in_=y0[:])
+        nc.sync.dma_start(out=out[:, 0:hi], in_=y0[:])
         y1 = keep.tile([P, hi], F32, name="y1")
         nc.vector.tensor_tensor(y1[:], ga[:, hi:I], gb1[:], MAX)
         nc.sync.dma_start(out=out[:, hi:I], in_=y1[:])

from contextlib import ExitStack

import concourse.mybir as mybir

D, T, U, I, O, L, Q = 512, 1024, 1024, 512, 2048, 1024, 128
FLOPS = 2 * D * Q * (T + U)

F32 = mybir.dt.float32
BF16 = mybir.dt.bfloat16
I32 = mybir.dt.int32
U32 = mybir.dt.uint32
U16 = mybir.dt.uint16
U8 = mybir.dt.uint8
FP8X4 = mybir.dt.float8_e4m3fn_x4
FP4X4 = mybir.dt.float4_e2m1fn_x4
COPY = mybir.ActivationFunctionType.Copy
SUB = mybir.AluOpType.subtract
MAX = mybir.AluOpType.max

P = 128
PACK = 4
N_TILE = 256
CACHE_ROW = 4
Q_VECTOR = 80
VECTOR_A = 768
VECTOR_B = 640


def tile_attend_endandback_two_kernel(
    tc, query, cache_words, cache_scales, draft_words, draft_scales, offs, offs2, offs3, offs4, out
):
    nc = tc.nc
    with ExitStack() as ctx:
        keep = ctx.enter_context(tc.tile_pool(name="keep", bufs=1))
        psum = ctx.enter_context(tc.psum_pool(name="psum", bufs=1))

        idx = keep.tile([P, L // 16], U16, name="idx")
        idx2 = keep.tile([P, L // 16], U16, name="idx2")
        idx3 = keep.tile([P, I // 16], U16, name="idx3")
        idx4 = keep.tile([P, I // 16], U16, name="idx4")

        draft_plane = keep.tile([P, U], U8, name="draft_plane", align_bytes=64)
        cache_plane = keep.tile([P, T], U8, name="cache_plane", align_bytes=64)
        nc.vector.memset(draft_plane[:].bitcast(I32), 0)
        nc.vector.memset(cache_plane[:].bitcast(I32), 0)

        q_raw = keep.tile([P, PACK, Q], F32, name="q_raw")
        nc.sync.dma_start(out=q_raw[:], in_=query.rearrange("(p j) q -> p j q", j=PACK))
        for r in range(4):
            nc.sync.dma_start(
                out=draft_plane[r:P:32, :].bitcast(I32), in_=draft_scales[0, r:16:4, :].bitcast(I32)
            )
        draft = keep.tile([P, 2 * U], U8, name="draft", align_bytes=64)
        nc.sync.dma_start(out=draft[:].bitcast(I32), in_=draft_words[0].bitcast(I32))
        cache = keep.tile([P, T], I32, name="cache", align_bytes=64)
        nc.sync.dma_start(out=cache[:], in_=cache_words[0].rearrange("p n t -> p (n t)").bitcast(I32))
        for r in range(4):
            nc.sync.dma_start(
                out=cache_plane[CACHE_ROW + r : P : 32, :].bitcast(I32),
                in_=cache_scales[0, r:16:4, :].bitcast(I32),
            )
        nc.sync.dma_start(idx[:], offs)
        nc.sync.dma_start(idx2[:], offs2)
        nc.sync.dma_start(idx3[:], offs3)
        nc.sync.dma_start(idx4[:], offs4)

        f1 = keep.tile([P, O], F32, name="f1")
        nc.vector.memset(f1[:], 0.0)

        q_bf = keep.tile([P, Q, PACK], BF16, name="q_bf", align_bytes=64)
        nc.vector.tensor_copy(
            out=q_bf[:, 0:Q_VECTOR, :].rearrange("p (c i) t -> p c t i", i=4),
            in_=q_raw[:, :, 0:Q_VECTOR].rearrange("p t (c i) -> p c t i", i=4),
        )
        nc.scalar.activation(
            q_bf[:, Q_VECTOR:Q, :].rearrange("p (c i) t -> p c t i", i=4),
            q_raw[:, :, Q_VECTOR:Q].rearrange("p t (c i) -> p c t i", i=4),
            COPY,
        )
        q_codes = keep.tile([P, Q], U32, name="q_codes", align_bytes=64)
        q_plane = keep.tile([P, Q], U8, name="q_plane", align_bytes=64)
        nc.vector.quantize_mx(
            out=q_codes[:].bitcast(FP8X4), scales=q_plane[:], in_=q_bf[:].rearrange("p q t -> p (q t)")
        )

        ab = keep.tile([P, O], F32, name="ab")
        banks = {}
        for s in range(O // N_TILE):
            acc = psum.tile([P, N_TILE], F32, name="acc%d" % s)
            if s < U // N_TILE:
                c = s * N_TILE
                rhs = draft[:, 2 * c : 2 * (c + N_TILE)].bitcast(FP4X4)
                rhs_scale = draft_plane[:, c : c + N_TILE]
                place = T + c
            else:
                c = s * N_TILE - U
                rhs = cache[:, c : c + N_TILE].bitcast(FP8X4)
                rhs_scale = cache_plane[CACHE_ROW:P, c : c + N_TILE]
                place = c
            nc.tensor.matmul_mx(
                out=acc[:],
                lhsT=q_codes[:].bitcast(FP8X4),
                lhsT_scale=q_plane[:],
                rhs=rhs,
                rhs_scale=rhs_scale,
                start=True,
                stop=True,
            )
            banks[place] = acc
            if s % 2 == 1:
                nc.scalar.activation(ab[:, place : place + N_TILE], acc[:], COPY)
            else:
                nc.vector.tensor_copy(ab[:, place : place + N_TILE], acc[:])

        half = L // 2
        picked = keep.tile([P, L], F32, name="picked")
        nc.scalar.activation(picked[:, 0:half], ab[:].indirect(idx[:, 0 : half // 16]), COPY)
        nc.vector.tensor_copy(picked[:, half:L], ab[:].indirect(idx[:, half // 16 : L // 16]))
        nc.scalar.activation(f1[:].indirect(idx2[:]), picked[:], COPY)

        aa = keep.tile([P, T], F32, name="aa")
        bb = keep.tile([P, U], F32, name="bb")
        for part, base, share in ((aa, 0, VECTOR_A), (bb, T, VECTOR_B)):
            nc.gpsimd.tensor_tensor(
                part[:, share:T], ab[:, base + share : base + T], f1[:, base + share : base + T], SUB
            )
            for c in range(0, share, N_TILE):
                n = min(N_TILE, share - c)
                nc.vector.tensor_tensor(
                    part[:, c : c + n], banks[base + c][:, 0:n], f1[:, base + c : base + c + n], SUB
                )

        ga = keep.tile([P, I], F32, name="ga")
        nc.scalar.activation(ga[:], aa[:].indirect(idx3[:]), COPY)
        hi = I // 2
        gb0 = keep.tile([P, hi], F32, name="gb0")
        gb1 = keep.tile([P, hi], F32, name="gb1")
        nc.scalar.activation(gb1[:], bb[:].indirect(idx4[:, hi // 16 : I // 16]), COPY)
        nc.vector.tensor_copy(gb0[:], bb[:].indirect(idx4[:, 0 : hi // 16]))
        y0 = keep.tile([P, hi], F32, name="y0")
        nc.vector.tensor_tensor(y0[:], ga[:, 0:hi], gb0[:], MAX)
        nc.sync.dma_start(out=out[:, 0:hi], in_=y0[:])
        y1 = keep.tile([P, hi], F32, name="y1")
        nc.vector.tensor_tensor(y1[:], ga[:, hi:I], gb1[:], MAX)
        nc.sync.dma_start(out=out[:, hi:I], in_=y1[:])
